import numpy as np
import ml_dtypes


def mxq(x, axis, fmt="e4m3"):
    dtype, down = {"e4m3": (ml_dtypes.float8_e4m3fn, 7), "e5m2": (ml_dtypes.float8_e5m2, 14)}[fmt]
    v = np.moveaxis(np.asarray(x, np.float32).astype(ml_dtypes.bfloat16).astype(np.float64), axis, -1)
    blocks = v.reshape(v.shape[:-1] + (-1, 32))
    amax = np.abs(blocks).max(-1, keepdims=True)
    byte = np.maximum(np.where(amax > 0, np.frexp(amax)[1] - 1 + 127, 0) - down, 1)
    scale = np.exp2(byte - 127.0)
    codes = (blocks / scale).astype(np.float32).astype(dtype).astype(np.float64)
    return np.moveaxis((codes * scale).reshape(v.shape), -1, axis)


WIDE = False


def mx_kscale(k):
    if not WIDE:
        return np.ones(k)
    levels = np.array([30, -30])
    if k % 512:
        return np.exp2(np.random.permutation(np.resize(levels, k // 32))).repeat(32)
    a = np.empty((k // 512, 16))
    for p in range(k // 512):
        a[p, :8] = np.random.permutation(np.resize(levels, 8))
        for g in range(8):
            far = levels[np.abs(levels - a[p, g]) >= 10]
            a[p, g + 8] = far[np.random.randint(len(far))]
    return np.exp2(a.ravel()).repeat(32)


def f64(x):
    return np.asarray(x).astype(np.float64)


def striped(idx):
    return np.tile(np.asarray(idx).reshape(-1, 16).T, (8, 1)).astype(np.uint16)


def unstriped(offs):
    return offs[:16].T.reshape(-1).astype(np.int64)


E2M1 = np.array([0.0, 0.5, 1.0, 1.5, 2.0, 3.0, 4.0, 6.0, -0.0, -0.5, -1.0, -1.5, -2.0, -3.0, -4.0, -6.0])


def pack_weight(w, fmt):
    k, n = w.shape
    w = f64(np.asarray(w, np.float32).astype(ml_dtypes.bfloat16)).reshape(k // 32, 32, n)
    amax = np.abs(w).max(1)
    if fmt in ("e4m3", "e5m2"):
        byte = np.frexp(amax)[1] - 1 + 127 - (7 if fmt == "e4m3" else 14)
    else:
        mant, ex = np.frexp(amax / 6.0)
        byte = np.where(mant > 0.5, ex, ex - 1) + 127
    byte = np.clip(np.where(amax > 0, byte, 1), 1, 254)
    scaled = (w * np.exp2(127.0 - byte)[:, None, :]).reshape(k, n).astype(np.float32)
    by_word = np.ascontiguousarray(scaled.reshape(k // 512, 128, 4, n).transpose(0, 1, 3, 2))
    if fmt in ("e4m3", "e5m2"):
        words = by_word.astype(ml_dtypes.float8_e4m3fn if fmt == "e4m3" else ml_dtypes.float8_e5m2).view(np.uint8)
    else:
        c = by_word.astype(ml_dtypes.float4_e2m1fn).view(np.uint8) & 0xF
        words = (c[..., 0::2] | (c[..., 1::2] << 4)).reshape(k // 512, 128, 2 * n)
    return np.ascontiguousarray(words), np.ascontiguousarray(byte.astype(np.uint8).reshape(k // 512, 16, n))


def unpack_weight(words, scales, fmt):
    g, _, n = scales.shape
    words = np.ascontiguousarray(words).reshape(g, 128, n, -1)
    if fmt in ("e4m3", "e5m2"):
        vals = words.view(ml_dtypes.float8_e4m3fn if fmt == "e4m3" else ml_dtypes.float8_e5m2).astype(np.float64)
    else:
        nib = np.empty((g, 128, n, 4), np.uint8)
        nib[..., 0::2] = words & 0xF
        nib[..., 1::2] = words >> 4
        vals = E2M1[nib]
    vals = vals * np.repeat(np.exp2(scales.astype(np.float64) - 127.0), 8, axis=1)[..., None]
    return vals.transpose(0, 1, 3, 2).reshape(g * 512, n)


K, T, J, R, C, O, N = 512, 1024, 256, 512, 512, 128, 256


def setup_inputs():
    n = np.random.standard_normal
    idx = np.random.permutation(T)[:J]
    idx2 = np.random.permutation(C)[:J]
    idx3 = np.random.permutation(C)[:O]
    idx4 = np.random.permutation(J)[:O]
    idx5 = np.random.permutation(T)[:O]
    fk = mx_kscale(K)
    fr = mx_kscale(R)
    xtp = pack_weight(n((K, T)) / fk[:, None], "e2m1")
    wp = pack_weight(n((K, R)) * 1 / np.sqrt(K) * fk[:, None] * fr, "e5m2")
    w2p = pack_weight(n((K, R)) * 1 / np.sqrt(K) * fk[:, None] * fr, "e4m3")
    wbp = pack_weight(n((R, N)) * 1 / np.sqrt(R) / fr[:, None], "e4m3")
    wsp = pack_weight(n((K, N)) * 1 / np.sqrt(K) * fk[:, None], "e4m3")
    return {
        "xt_words": xtp[0],
        "xt_scales": xtp[1],
        "w_words": wp[0],
        "w_scales": wp[1],
        "w2_words": w2p[0],
        "w2_scales": w2p[1],
        "sa": (np.random.uniform(0.5, 1.6, (R, 1))).astype(np.float32),
        "wb_words": wbp[0],
        "wb_scales": wbp[1],
        "ws_words": wsp[0],
        "ws_scales": wsp[1],
        "offs": striped(idx),
        "offs2": striped(idx2),
        "offs3": striped(idx3),
        "offs4": striped(idx4),
        "offs5": striped(idx5),
    }


def reference(xt_words, xt_scales, w_words, w_scales, w2_words, w2_scales, sa, wb_words, wb_scales, ws_words, ws_scales, offs, offs2, offs3, offs4, offs5):
    idx = unstriped(offs)
    idx2 = unstriped(offs2)
    idx3 = unstriped(offs3)
    idx4 = unstriped(offs4)
    idx5 = unstriped(offs5)
    xtu = unpack_weight(xt_words, xt_scales, "e2m1")
    wu = unpack_weight(w_words, w_scales, "e5m2")
    w2u = unpack_weight(w2_words, w2_scales, "e4m3")
    wbu = unpack_weight(wb_words, wb_scales, "e4m3")
    wsu = unpack_weight(ws_words, ws_scales, "e4m3")
    xtidxg = xtu[:, idx]
    a = wu.T @ xtidxg
    b = w2u.T @ xtidxg
    pw = np.zeros((R, C))
    pw[:, idx2] = a
    hid = np.maximum(pw[:, idx3] * f64(sa), b[:, idx4])
    hidq = mxq(hid, 0, "e5m2")
    xtidx5g = xtu[:, idx5]
    y = wbu.T @ hidq + wsu.T @ xtidx5g
    return y

@@ -1,0 +1,194 @@
+from contextlib import ExitStack
+
+import concourse.mybir as mybir
+
+K, T, J, R, C, O, N = 512, 1024, 256, 512, 512, 128, 256
+FLOPS = 2 * K * R * J * 2 + 2 * R * N * O + 2 * K * N * O
+
+F32 = mybir.dt.float32
+BF16 = mybir.dt.bfloat16
+I32 = mybir.dt.int32
+U32 = mybir.dt.uint32
+U16 = mybir.dt.uint16
+U8 = mybir.dt.uint8
+E4M3 = mybir.dt.float8_e4m3fn_x4
+E5M2 = mybir.dt.float8_e5m2_x4
+E2M1 = mybir.dt.float4_e2m1fn_x4
+COPY = mybir.ActivationFunctionType.Copy
+MAX = mybir.AluOpType.max
+
+P = 128
+PACK = 4
+
+
+def load_words(nc, tile, words):
+    nc.sync.dma_start(out=tile[:].bitcast(I32), in_=words[0].rearrange("p n t -> p (n t)").bitcast(I32))
+
+
+def load_scales_in_halves(nc, tile, scales):
+    rows = scales[0].bitcast(I32).rearrange("(h q r) c -> q r h c", h=2, q=2)
+    for q in range(2):
+        nc.sync.dma_start(
+            out=tile[32 * q : 32 * q + 4, :].bitcast(I32).rearrange("r (h c) -> r h c", h=2), in_=rows[q]
+        )
+
+
+def lift_upper_half(nc, plane, tile, width):
+    nc.vector.tensor_copy(out=plane[64:128, 0:width].bitcast(I32), in_=tile[0:64, width : 2 * width].bitcast(I32))
+
+
+def load_scales_in_place(nc, tile, cols, scales):
+    for q in range(4):
+        nc.sync.dma_start(
+            out=tile[32 * q : 32 * q + 4, cols].bitcast(I32), in_=scales[0, 4 * q : 4 * q + 4, :].bitcast(I32)
+        )
+
+
+def dealt_views(dst, src, run):
+    return (
+        dst.rearrange("p (t c i) -> p c t i", t=PACK, i=run),
+        src.rearrange("p (c i t) -> p c t i", t=PACK, i=run),
+    )
+
+
+def tile_list_boardweighed_twow_further_plain_kernel(
+    tc, xt_words, xt_scales, w_words, w_scales, w2_words, w2_scales, sa, wb_words, wb_scales,
+    ws_words, ws_scales, offs, offs2, offs3, offs4, offs5, out,
+):
+    nc = tc.nc
+    with ExitStack() as ctx:
+        lists = ctx.enter_context(tc.tile_pool(name="lists", bufs=1))
+        sb = ctx.enter_context(tc.tile_pool(name="sb", bufs=1))
+        psum = ctx.enter_context(tc.psum_pool(name="psum", bufs=1))
+
+        l1 = lists.tile([P, J // 16], U16, name="l1")
+        l2 = lists.tile([P, J // 16], U16, name="l2")
+        l3 = lists.tile([P, O // 16], U16, name="l3")
+        l4 = lists.tile([P, O // 16], U16, name="l4")
+        l5 = lists.tile([P, O // 16], U16, name="l5")
+
+        xw = sb.tile([P, T], U16, name="xw", align_bytes=64)
+        xs_halves = sb.tile([64, 2 * T], U8, name="xs_halves", align_bytes=64)
+        xs = sb.tile([P, T], U8, name="xs", align_bytes=64)
+        ww = sb.tile([P, R], U32, name="ww", align_bytes=64)
+        wsc = sb.tile([P, 2 * R], U8, name="wsc", align_bytes=64)
+        w2w = sb.tile([P, R], U32, name="w2w", align_bytes=64)
+        late = sb.tile([P, R + 2 * N], U8, name="late", align_bytes=64)
+        w2_cols, ws_cols, wb_cols = slice(0, R), slice(R, R + N), slice(R + N, R + 2 * N)
+        wbw = sb.tile([P, N], U32, name="wbw", align_bytes=64)
+        wsw = sb.tile([P, N], U32, name="wsw", align_bytes=64)
+        sat = sb.tile([P, PACK], F32, name="sat", align_bytes=64)
+        board = [sb.tile([P, C], F32, name="board%d" % t, align_bytes=64) for t in range(PACK)]
+
+        nc.vector.memset(xs_halves[:].bitcast(I32), 0)
+        nc.gpsimd.memset(wsc[:].bitcast(I32), 0)
+        nc.gpsimd.memset(late[:].bitcast(I32), 0)
+
+        nc.sync.dma_start(l1[:], offs)
+        nc.sync.dma_start(out=xw[:].bitcast(I32), in_=xt_words[0].bitcast(I32))
+        load_scales_in_halves(nc, xs_halves, xt_scales)
+        load_words(nc, ww, w_words)
+        load_scales_in_halves(nc, wsc, w_scales)
+        load_words(nc, w2w, w2_words)
+        nc.sync.dma_start(l5[:], offs5)
+        nc.sync.dma_start(l2[:], offs2)
+        load_scales_in_place(nc, late, w2_cols, w2_scales)
+        nc.sync.dma_start(l3[:], offs3)
+        nc.sync.dma_start(out=sat[:], in_=sa.rearrange("(p t) u -> p (t u)", t=PACK))
+        nc.sync.dma_start(l4[:], offs4)
+        load_words(nc, wsw, ws_words)
+        load_scales_in_place(nc, late, ws_cols, ws_scales)
+        load_words(nc, wbw, wb_words)
+        load_scales_in_place(nc, late, wb_cols, wb_scales)
+
+        xgw = sb.tile([P, J], U16, name="xgw", align_bytes=64)
+        xgs = sb.tile([P, J], U8, name="xgs", align_bytes=64)
+        x5w = sb.tile([P, O], U16, name="x5w", align_bytes=64)
+        x5s = sb.tile([P, O], U8, name="x5s", align_bytes=64)
+        wd = sb.tile([P, R], U32, name="wd", align_bytes=64)
+        wds = sb.tile([P, R], U8, name="wds", align_bytes=64)
+        w2d = sb.tile([P, R], U32, name="w2d", align_bytes=64)
+        w2ds = sb.tile([P, R], U8, name="w2ds", align_bytes=64)
+
+        nc.vector.tensor_copy(out=xs[0:64, :].bitcast(I32), in_=xs_halves[:, 0:T].bitcast(I32))
+        lift_upper_half(nc, xs, xs_halves, T)
+        lift_upper_half(nc, wsc, wsc, R)
+        nc.vector.tensor_copy(xgs[:], xs[:].indirect(l1[:]))
+        dst, src = dealt_views(wds[:], wsc[:, 0:R], 16)
+        nc.vector.tensor_copy(out=dst, in_=src)
+        nc.vector.tensor_copy(xgw[:], xw[:].indirect(l1[:]))
+        dst, src = dealt_views(wd[:], ww[:], 4)
+        nc.scalar.copy(out=dst, in_=src)
+        dst, src = dealt_views(w2d[:], w2w[:], 4)
+        nc.scalar.copy(out=dst, in_=src)
+        dst, src = dealt_views(w2ds[:], late[:, w2_cols], 16)
+        nc.gpsimd.tensor_copy(out=dst, in_=src)
+
+        a_ps = [psum.tile([P, J], F32, name="a_ps%d" % t) for t in range(PACK)]
+        b_ps = [psum.tile([P, 2 * J], F32, name="b_ps%d" % h) for h in range(2)]
+        y_ps = [psum.tile([P, O], F32, name="y_ps%d" % h) for h in range(2)]
+        for t in range(PACK):
+            cols = slice(P * t, P * (t + 1))
+            nc.tensor.matmul_mx(
+                out=a_ps[t][:], lhsT=wd[:, cols].bitcast(E5M2), lhsT_scale=wds[:, cols],
+                rhs=xgw[:].bitcast(E2M1), rhs_scale=xgs[:], start=True, stop=True,
+            )
+        for t in range(PACK):
+            cols = slice(P * t, P * (t + 1))
+            nc.tensor.matmul_mx(
+                out=b_ps[t // 2][:, J * (t % 2) : J * (t % 2 + 1)], lhsT=w2d[:, cols].bitcast(E4M3),
+                lhsT_scale=w2ds[:, cols], rhs=xgw[:].bitcast(E2M1), rhs_scale=xgs[:], start=True, stop=True,
+            )
+
+        nc.vector.tensor_copy(x5w[:], xw[:].indirect(l5[:]))
+        nc.vector.tensor_copy(x5s[:], xs[:].indirect(l5[:]))
+        for h in range(2):
+            cols = slice(P * h, P * (h + 1))
+            nc.tensor.matmul_mx(
+                out=y_ps[h][:], lhsT=wsw[:, cols].bitcast(E4M3), lhsT_scale=late[:, R + P * h : R + P * (h + 1)],
+                rhs=x5w[:].bitcast(E2M1), rhs_scale=x5s[:], start=True, stop=False,
+            )
+
+        for t in range(PACK):
+            nc.vector.memset(board[t][:], 0.0)
+
+        a_sb = [sb.tile([P, J], F32, name="a_sb%d" % t, align_bytes=64) for t in range(PACK)]
+        b_sb = [sb.tile([P, 2 * J], F32, name="b_sb%d" % h, align_bytes=64) for h in range(2)]
+        picked_a = sb.tile([P, PACK, O], F32, name="picked_a", align_bytes=64)
+        picked_b = sb.tile([P, PACK, O], F32, name="picked_b", align_bytes=64)
+
+        for t in (0, 2):
+            nc.scalar.copy(out=a_sb[t][:], in_=a_ps[t][:])
+            nc.vector.tensor_copy(out=a_sb[t + 1][:], in_=a_ps[t + 1][:])
+        for t in (0, 2):
+            nc.scalar.activation(board[t][:].indirect(l2[:]), a_sb[t][:], COPY)
+            nc.vector.tensor_copy(board[t + 1][:].indirect(l2[:]), a_sb[t + 1][:])
+        for h in range(2):
+            nc.scalar.copy(out=b_sb[h][:], in_=b_ps[h][:])
+        for t in range(PACK):
+            nc.vector.tensor_copy(picked_b[:, t, :], b_sb[t // 2][:, J * (t % 2) : J * (t % 2 + 1)].indirect(l4[:]))
+        for t in (0, 2, 1, 3):
+            nc.scalar.activation(picked_a[:, t, :], board[t][:].indirect(l3[:]), COPY, scale=sat[:, t : t + 1])
+
+        hid = sb.tile([P, O * PACK], BF16, name="hid", align_bytes=64)
+        hq = sb.tile([P, O], U32, name="hq", align_bytes=64)
+        hs = sb.tile([P, O], U8, name="hs", align_bytes=64)
+        nc.vector.tensor_tensor(
+            out=hid[:].rearrange("p (c i t) -> p c t i", i=4, t=PACK),
+            in0=picked_a[:].rearrange("p t (c i) -> p c t i", i=4),
+            in1=picked_b[:].rearrange("p t (c i) -> p c t i", i=4),
+            op=MAX,
+        )
+        nc.vector.quantize_mx(out=hq[:].bitcast(E5M2), scales=hs[:], in_=hid[:])
+
+        y_sb = [sb.tile([P, O], F32, name="y_sb%d" % h, align_bytes=64) for h in range(2)]
+        for h in range(2):
+            cols = slice(P * h, P * (h + 1))
+            nc.tensor.matmul_mx(
+                out=y_ps[h][:], lhsT=wbw[:, cols].bitcast(E4M3), lhsT_scale=late[:, R + N + P * h : R + N + P * (h + 1)],
+                rhs=hq[:].bitcast(E5M2), rhs_scale=hs[:], start=False, stop=True,
+            )
+        nc.vector.tensor_copy(out=y_sb[0][:], in_=y_ps[0][:])
+        nc.sync.dma_start(out=out[0:P, :], in_=y_sb[0][:])
+        nc.scalar.copy(out=y_sb[1][:], in_=y_ps[1][:])
+        nc.scalar.dma_start(out=out[P : 2 * P, :], in_=y_sb[1][:])

@@ -25,16 +25,18 @@ def load_words(nc, tile, words):
     nc.sync.dma_start(out=tile[:].bitcast(I32), in_=words[0].rearrange("p n t -> p (n t)").bitcast(I32))
 
 
-def load_scales_in_halves(nc, tile, scales):
-    rows = scales[0].bitcast(I32).rearrange("(h q r) c -> q r h c", h=2, q=2)
-    for q in range(2):
-        nc.sync.dma_start(
-            out=tile[32 * q : 32 * q + 4, :].bitcast(I32).rearrange("r (h c) -> r h c", h=2), in_=rows[q]
+def load_scales_side_by_side(nc, tile, scales):
+    nc.sync.dma_start(
+        out=tile[:].bitcast(I32).rearrange("r (q c) -> r q c", q=4),
+        in_=scales[0].bitcast(I32).rearrange("(q r) c -> r q c", q=4),
+    )
+
+
+def spread_scales(nc, plane, tile, width):
+    for q in range(4):
+        nc.vector.tensor_copy(
+            out=plane[32 * q : 32 * q + 4, :].bitcast(I32), in_=tile[:, width * q : width * (q + 1)].bitcast(I32)
         )
-
-
-def lift_upper_half(nc, plane, tile, width):
-    nc.vector.tensor_copy(out=plane[64:128, 0:width].bitcast(I32), in_=tile[0:64, width : 2 * width].bitcast(I32))
 
 
 def load_scales_in_place(nc, tile, cols, scales):
@@ -68,27 +70,27 @@ def tile_list_boardweighed_twow_further_plain_kernel(
         l5 = lists.tile([P, O // 16], U16, name="l5")
 
         xw = sb.tile([P, T], U16, name="xw", align_bytes=64)
-        xs_halves = sb.tile([64, 2 * T], U8, name="xs_halves", align_bytes=64)
         xs = sb.tile([P, T], U8, name="xs", align_bytes=64)
-        ww = sb.tile([P, R], U32, name="ww", align_bytes=64)
-        wsc = sb.tile([P, 2 * R], U8, name="wsc", align_bytes=64)
+        ww = sb.tile([P, R], U32, name="ww", tag="ww_then_board3", align_bytes=64)
+        wsc_rows = sb.tile([4, 4 * R], U8, name="wsc_rows", align_bytes=64)
+        wsc = sb.tile([P, R], U8, name="wsc", tag="wsc_then_board2", align_bytes=64)
         w2w = sb.tile([P, R], U32, name="w2w", align_bytes=64)
         late = sb.tile([P, R + 2 * N], U8, name="late", align_bytes=64)
         w2_cols, ws_cols, wb_cols = slice(0, R), slice(R, R + N), slice(R + N, R + 2 * N)
         wbw = sb.tile([P, N], U32, name="wbw", align_bytes=64)
         wsw = sb.tile([P, N], U32, name="wsw", align_bytes=64)
         sat = sb.tile([P, PACK], F32, name="sat", align_bytes=64)
-        board = [sb.tile([P, C], F32, name="board%d" % t, align_bytes=64) for t in range(PACK)]
 
-        nc.vector.memset(xs_halves[:].bitcast(I32), 0)
-        nc.gpsimd.memset(wsc[:].bitcast(I32), 0)
+        nc.vector.memset(xs[:, 0 : T // 2].bitcast(I32), 0)
+        nc.gpsimd.memset(xs[:, T // 2 : T].bitcast(I32), 0)
+        nc.vector.memset(wsc[:].bitcast(I32), 0)
         nc.gpsimd.memset(late[:].bitcast(I32), 0)
 
         nc.sync.dma_start(l1[:], offs)
+        load_scales_side_by_side(nc, wsc_rows, w_scales)
+        load_scales_in_place(nc, xs, slice(0, T), xt_scales)
         nc.sync.dma_start(out=xw[:].bitcast(I32), in_=xt_words[0].bitcast(I32))
-        load_scales_in_halves(nc, xs_halves, xt_scales)
         load_words(nc, ww, w_words)
-        load_scales_in_halves(nc, wsc, w_scales)
         load_words(nc, w2w, w2_words)
         nc.sync.dma_start(l5[:], offs5)
         nc.sync.dma_start(l2[:], offs2)
@@ -107,18 +109,18 @@ def tile_list_boardweighed_twow_further_plain_kernel(
         x5s = sb.tile([P, O], U8, name="x5s", align_bytes=64)
         wd = sb.tile([P, R], U32, name="wd", align_bytes=64)
         wds = sb.tile([P, R], U8, name="wds", align_bytes=64)
-        w2d = sb.tile([P, R], U32, name="w2d", align_bytes=64)
+        w2d = sb.tile([P, R], U32, name="w2d", tag="w2d_then_picked_a", align_bytes=64)
         w2ds = sb.tile([P, R], U8, name="w2ds", align_bytes=64)
 
-        nc.vector.tensor_copy(out=xs[0:64, :].bitcast(I32), in_=xs_halves[:, 0:T].bitcast(I32))
-        lift_upper_half(nc, xs, xs_halves, T)
-        lift_upper_half(nc, wsc, wsc, R)
-        nc.vector.tensor_copy(xgs[:], xs[:].indirect(l1[:]))
-        dst, src = dealt_views(wds[:], wsc[:, 0:R], 16)
-        nc.vector.tensor_copy(out=dst, in_=src)
+        spread_scales(nc, wsc, wsc_rows, R)
+        dst, src = dealt_views(wds[:], wsc[:], 16)
+        nc.vector.tensor_copy(out=dst[:, :, 0:2, :], in_=src[:, :, 0:2, :])
+        nc.gpsimd.tensor_copy(out=dst[:, :, 2:4, :], in_=src[:, :, 2:4, :])
         nc.vector.tensor_copy(xgw[:], xw[:].indirect(l1[:]))
+        nc.vector.tensor_copy(xgs[:], xs[:].indirect(l1[:]))
         dst, src = dealt_views(wd[:], ww[:], 4)
-        nc.scalar.copy(out=dst, in_=src)
+        nc.scalar.copy(out=dst[:, :, 0:2, :], in_=src[:, :, 0:2, :])
+        nc.scalar.copy(out=dst[:, :, 2:4, :], in_=src[:, :, 2:4, :])
         dst, src = dealt_views(w2d[:], w2w[:], 4)
         nc.scalar.copy(out=dst, in_=src)
         dst, src = dealt_views(w2ds[:], late[:, w2_cols], 16)
@@ -149,12 +151,15 @@ def tile_list_boardweighed_twow_further_plain_kernel(
                 rhs=x5w[:].bitcast(E2M1), rhs_scale=x5s[:], start=True, stop=False,
             )
 
-        for t in range(PACK):
+        board_tags = ("board0", "board1", "wsc_then_board2", "ww_then_board3")
+        board = [sb.tile([P, C], F32, name="board%d" % t, tag=board_tags[t], align_bytes=64) for t in range(PACK)]
+        for t in range(2):
             nc.vector.memset(board[t][:], 0.0)
+            nc.gpsimd.memset(board[t + 2][:], 0.0)
 
         a_sb = [sb.tile([P, J], F32, name="a_sb%d" % t, align_bytes=64) for t in range(PACK)]
         b_sb = [sb.tile([P, 2 * J], F32, name="b_sb%d" % h, align_bytes=64) for h in range(2)]
-        picked_a = sb.tile([P, PACK, O], F32, name="picked_a", align_bytes=64)
+        picked_a = sb.tile([P, PACK, O], F32, name="picked_a", tag="w2d_then_picked_a", align_bytes=64)
         picked_b = sb.tile([P, PACK, O], F32, name="picked_b", align_bytes=64)
 
         for t in (0, 2):
@@ -163,8 +168,8 @@ def tile_list_boardweighed_twow_further_plain_kernel(
         for t in (0, 2):
             nc.scalar.activation(board[t][:].indirect(l2[:]), a_sb[t][:], COPY)
             nc.vector.tensor_copy(board[t + 1][:].indirect(l2[:]), a_sb[t + 1][:])
-        for h in range(2):
-            nc.scalar.copy(out=b_sb[h][:], in_=b_ps[h][:])
+        nc.scalar.copy(out=b_sb[0][:], in_=b_ps[0][:])
+        nc.vector.tensor_copy(out=b_sb[1][:], in_=b_ps[1][:])
         for t in range(PACK):
             nc.vector.tensor_copy(picked_b[:, t, :], b_sb[t // 2][:, J * (t % 2) : J * (t % 2 + 1)].indirect(l4[:]))
         for t in (0, 2, 1, 3):

@@ -71,9 +71,9 @@ def tile_list_boardweighed_twow_further_plain_kernel(
 
         xw = sb.tile([P, T], U16, name="xw", align_bytes=64)
         xs = sb.tile([P, T], U8, name="xs", align_bytes=64)
-        ww = sb.tile([P, R], U32, name="ww", tag="ww_then_board3", align_bytes=64)
+        ww = sb.tile([P, R], U32, name="ww", align_bytes=64)
         wsc_rows = sb.tile([4, 4 * R], U8, name="wsc_rows", align_bytes=64)
-        wsc = sb.tile([P, R], U8, name="wsc", tag="wsc_then_board2", align_bytes=64)
+        wsc = sb.tile([P, R], U8, name="wsc", align_bytes=64)
         w2w = sb.tile([P, R], U32, name="w2w", align_bytes=64)
         late = sb.tile([P, R + 2 * N], U8, name="late", align_bytes=64)
         w2_cols, ws_cols, wb_cols = slice(0, R), slice(R, R + N), slice(R + N, R + 2 * N)
@@ -88,13 +88,13 @@ def tile_list_boardweighed_twow_further_plain_kernel(
 
         nc.sync.dma_start(l1[:], offs)
         load_scales_side_by_side(nc, wsc_rows, w_scales)
-        load_scales_in_place(nc, xs, slice(0, T), xt_scales)
         nc.sync.dma_start(out=xw[:].bitcast(I32), in_=xt_words[0].bitcast(I32))
         load_words(nc, ww, w_words)
-        load_words(nc, w2w, w2_words)
-        nc.sync.dma_start(l5[:], offs5)
+        load_scales_in_place(nc, xs, slice(0, T), xt_scales)
         nc.sync.dma_start(l2[:], offs2)
+        load_words(nc, w2w, w2_words)
         load_scales_in_place(nc, late, w2_cols, w2_scales)
+        nc.sync.dma_start(l5[:], offs5)
         nc.sync.dma_start(l3[:], offs3)
         nc.sync.dma_start(out=sat[:], in_=sa.rearrange("(p t) u -> p (t u)", t=PACK))
         nc.sync.dma_start(l4[:], offs4)
@@ -105,11 +105,9 @@ def tile_list_boardweighed_twow_further_plain_kernel(
 
         xgw = sb.tile([P, J], U16, name="xgw", align_bytes=64)
         xgs = sb.tile([P, J], U8, name="xgs", align_bytes=64)
-        x5w = sb.tile([P, O], U16, name="x5w", align_bytes=64)
-        x5s = sb.tile([P, O], U8, name="x5s", align_bytes=64)
         wd = sb.tile([P, R], U32, name="wd", align_bytes=64)
         wds = sb.tile([P, R], U8, name="wds", align_bytes=64)
-        w2d = sb.tile([P, R], U32, name="w2d", tag="w2d_then_picked_a", align_bytes=64)
+        w2d = sb.tile([P, R], U32, name="w2d", tag="w2d_then_x5w", align_bytes=64)
         w2ds = sb.tile([P, R], U8, name="w2ds", align_bytes=64)
 
         spread_scales(nc, wsc, wsc_rows, R)
@@ -121,10 +119,11 @@ def tile_list_boardweighed_twow_further_plain_kernel(
         dst, src = dealt_views(wd[:], ww[:], 4)
         nc.scalar.copy(out=dst[:, :, 0:2, :], in_=src[:, :, 0:2, :])
         nc.scalar.copy(out=dst[:, :, 2:4, :], in_=src[:, :, 2:4, :])
-        dst, src = dealt_views(w2d[:], w2w[:], 4)
-        nc.scalar.copy(out=dst, in_=src)
-        dst, src = dealt_views(w2ds[:], late[:, w2_cols], 16)
-        nc.gpsimd.tensor_copy(out=dst, in_=src)
+        for pair in (slice(0, 2), slice(2, 4)):
+            dst, src = dealt_views(w2ds[:], late[:, w2_cols], 16)
+            nc.gpsimd.tensor_copy(out=dst[:, :, pair, :], in_=src[:, :, pair, :])
+            dst, src = dealt_views(w2d[:], w2w[:], 4)
+            nc.gpsimd.tensor_copy(out=dst[:, :, pair, :], in_=src[:, :, pair, :])
 
         a_ps = [psum.tile([P, J], F32, name="a_ps%d" % t) for t in range(PACK)]
         b_ps = [psum.tile([P, 2 * J], F32, name="b_ps%d" % h) for h in range(2)]
@@ -142,6 +141,33 @@ def tile_list_boardweighed_twow_further_plain_kernel(
                 lhsT_scale=w2ds[:, cols], rhs=xgw[:].bitcast(E2M1), rhs_scale=xgs[:], start=True, stop=True,
             )
 
+        board = [sb.tile([P, C], F32, name="board%d" % t, align_bytes=64) for t in range(PACK)]
+        for t in range(2):
+            nc.vector.memset(board[t][:], 0.0)
+            nc.gpsimd.memset(board[t + 2][:], 0.0)
+
+        a_sb = [sb.tile([P, J], F32, name="a_sb%d" % t, align_bytes=64) for t in range(PACK)]
+        b_sb = [sb.tile([P, 2 * J], F32, name="b_sb%d" % h, align_bytes=64) for h in range(2)]
+        picked_a = sb.tile([P, PACK, O], F32, name="picked_a", align_bytes=64)
+        picked_b = sb.tile([P, PACK, O], F32, name="picked_b", align_bytes=64)
+
+        for t in (0, 2):
+            nc.vector.tensor_copy(out=a_sb[t][:], in_=a_ps[t][:])
+            nc.scalar.copy(out=a_sb[t + 1][:], in_=a_ps[t + 1][:])
+        for t in (0, 2):
+            nc.vector.tensor_copy(board[t][:].indirect(l2[:]), a_sb[t][:])
+            nc.scalar.activation(board[t + 1][:].indirect(l2[:]), a_sb[t + 1][:], COPY)
+        for h in range(2):
+            nc.vector.tensor_copy(out=b_sb[h][:], in_=b_ps[h][:])
+        for t in (1, 3, 0, 2):
+            nc.scalar.activation(picked_a[:, t, :], board[t][:].indirect(l3[:]), COPY, scale=sat[:, t : t + 1])
+        for u in range(2):
+            window = slice(J * u, J * (u + 1))
+            nc.scalar.activation(picked_b[:, u, :], b_sb[0][:, window].indirect(l4[:]), COPY)
+            nc.vector.tensor_copy(picked_b[:, 2 + u, :], b_sb[1][:, window].indirect(l4[:]))
+
+        x5w = sb.tile([P, O], U16, name="x5w", tag="w2d_then_x5w", align_bytes=64)
+        x5s = sb.tile([P, O], U8, name="x5s", tag="b_sb1", align_bytes=64)
         nc.vector.tensor_copy(x5w[:], xw[:].indirect(l5[:]))
         nc.vector.tensor_copy(x5s[:], xs[:].indirect(l5[:]))
         for h in range(2):
@@ -151,40 +177,21 @@ def tile_list_boardweighed_twow_further_plain_kernel(
                 rhs=x5w[:].bitcast(E2M1), rhs_scale=x5s[:], start=True, stop=False,
             )
 
-        board_tags = ("board0", "board1", "wsc_then_board2", "ww_then_board3")
-        board = [sb.tile([P, C], F32, name="board%d" % t, tag=board_tags[t], align_bytes=64) for t in range(PACK)]
-        for t in range(2):
-            nc.vector.memset(board[t][:], 0.0)
-            nc.gpsimd.memset(board[t + 2][:], 0.0)
-
-        a_sb = [sb.tile([P, J], F32, name="a_sb%d" % t, align_bytes=64) for t in range(PACK)]
-        b_sb = [sb.tile([P, 2 * J], F32, name="b_sb%d" % h, align_bytes=64) for h in range(2)]
-        picked_a = sb.tile([P, PACK, O], F32, name="picked_a", tag="w2d_then_picked_a", align_bytes=64)
-        picked_b = sb.tile([P, PACK, O], F32, name="picked_b", align_bytes=64)
-
-        for t in (0, 2):
-            nc.scalar.copy(out=a_sb[t][:], in_=a_ps[t][:])
-            nc.vector.tensor_copy(out=a_sb[t + 1][:], in_=a_ps[t + 1][:])
-        for t in (0, 2):
-            nc.scalar.activation(board[t][:].indirect(l2[:]), a_sb[t][:], COPY)
-            nc.vector.tensor_copy(board[t + 1][:].indirect(l2[:]), a_sb[t + 1][:])
-        nc.scalar.copy(out=b_sb[0][:], in_=b_ps[0][:])
-        nc.vector.tensor_copy(out=b_sb[1][:], in_=b_ps[1][:])
-        for t in range(PACK):
-            nc.vector.tensor_copy(picked_b[:, t, :], b_sb[t // 2][:, J * (t % 2) : J * (t % 2 + 1)].indirect(l4[:]))
-        for t in (0, 2, 1, 3):
-            nc.scalar.activation(picked_a[:, t, :], board[t][:].indirect(l3[:]), COPY, scale=sat[:, t : t + 1])
-
         hid = sb.tile([P, O * PACK], BF16, name="hid", align_bytes=64)
         hq = sb.tile([P, O], U32, name="hq", align_bytes=64)
         hs = sb.tile([P, O], U8, name="hs", align_bytes=64)
-        nc.vector.tensor_tensor(
-            out=hid[:].rearrange("p (c i t) -> p c t i", i=4, t=PACK),
-            in0=picked_a[:].rearrange("p t (c i) -> p c t i", i=4),
-            in1=picked_b[:].rearrange("p t (c i) -> p c t i", i=4),
-            op=MAX,
-        )
-        nc.vector.quantize_mx(out=hq[:].bitcast(E5M2), scales=hs[:], in_=hid[:])
+        halves = (slice(0, O // 2), slice(O // 2, O))
+        for half in halves:
+            nc.vector.tensor_tensor(
+                out=hid[:, PACK * half.start : PACK * half.stop].rearrange("p (c i t) -> p c t i", i=2, t=PACK),
+                in0=picked_a[:, :, half].rearrange("p t (c i) -> p c t i", i=2),
+                in1=picked_b[:, :, half].rearrange("p t (c i) -> p c t i", i=2),
+                op=MAX,
+            )
+        for half in halves:
+            nc.vector.quantize_mx(
+                out=hq[:, half].bitcast(E5M2), scales=hs[:, half], in_=hid[:, PACK * half.start : PACK * half.stop]
+            )
 
         y_sb = [sb.tile([P, O], F32, name="y_sb%d" % h, align_bytes=64) for h in range(2)]
         for h in range(2):

@@ -83,16 +83,16 @@ def tile_list_boardweighed_twow_further_plain_kernel(
 
         nc.vector.memset(xs[:, 0 : T // 2].bitcast(I32), 0)
         nc.gpsimd.memset(xs[:, T // 2 : T].bitcast(I32), 0)
-        nc.vector.memset(wsc[:].bitcast(I32), 0)
-        nc.gpsimd.memset(late[:].bitcast(I32), 0)
+        for plane in (wsc, late):
+            nc.vector.memset(plane[:].bitcast(I32), 0)
 
         nc.sync.dma_start(l1[:], offs)
         load_scales_side_by_side(nc, wsc_rows, w_scales)
         nc.sync.dma_start(out=xw[:].bitcast(I32), in_=xt_words[0].bitcast(I32))
         load_words(nc, ww, w_words)
         load_scales_in_place(nc, xs, slice(0, T), xt_scales)
-        nc.sync.dma_start(l2[:], offs2)
         load_words(nc, w2w, w2_words)
+        nc.sync.dma_start(l2[:], offs2)
         load_scales_in_place(nc, late, w2_cols, w2_scales)
         nc.sync.dma_start(l5[:], offs5)
         nc.sync.dma_start(l3[:], offs3)
@@ -119,11 +119,12 @@ def tile_list_boardweighed_twow_further_plain_kernel(
         dst, src = dealt_views(wd[:], ww[:], 4)
         nc.scalar.copy(out=dst[:, :, 0:2, :], in_=src[:, :, 0:2, :])
         nc.scalar.copy(out=dst[:, :, 2:4, :], in_=src[:, :, 2:4, :])
-        for pair in (slice(0, 2), slice(2, 4)):
-            dst, src = dealt_views(w2ds[:], late[:, w2_cols], 16)
-            nc.gpsimd.tensor_copy(out=dst[:, :, pair, :], in_=src[:, :, pair, :])
-            dst, src = dealt_views(w2d[:], w2w[:], 4)
-            nc.gpsimd.tensor_copy(out=dst[:, :, pair, :], in_=src[:, :, pair, :])
+        dst, src = dealt_views(w2d[:], w2w[:], 4)
+        nc.scalar.copy(out=dst[:, :, 0:2, :], in_=src[:, :, 0:2, :])
+        nc.gpsimd.tensor_copy(out=dst[:, :, 2:4, :], in_=src[:, :, 2:4, :])
+        dst, src = dealt_views(w2ds[:], late[:, w2_cols], 16)
+        nc.gpsimd.tensor_copy(out=dst[:, :, 0:2, :], in_=src[:, :, 0:2, :])
+        nc.gpsimd.tensor_copy(out=dst[:, :, 2:4, :], in_=src[:, :, 2:4, :])
 
         a_ps = [psum.tile([P, J], F32, name="a_ps%d" % t) for t in range(PACK)]
         b_ps = [psum.tile([P, 2 * J], F32, name="b_ps%d" % h) for h in range(2)]
@@ -142,9 +143,8 @@ def tile_list_boardweighed_twow_further_plain_kernel(
             )
 
         board = [sb.tile([P, C], F32, name="board%d" % t, align_bytes=64) for t in range(PACK)]
-        for t in range(2):
+        for t in range(PACK):
             nc.vector.memset(board[t][:], 0.0)
-            nc.gpsimd.memset(board[t + 2][:], 0.0)
 
         a_sb = [sb.tile([P, J], F32, name="a_sb%d" % t, align_bytes=64) for t in range(PACK)]
         b_sb = [sb.tile([P, 2 * J], F32, name="b_sb%d" % h, align_bytes=64) for h in range(2)]

from contextlib import ExitStack

import concourse.mybir as mybir

K, T, J, R, C, O, N = 512, 1024, 256, 512, 512, 128, 256
FLOPS = 2 * K * R * J * 2 + 2 * R * N * O + 2 * K * N * O

F32 = mybir.dt.float32
BF16 = mybir.dt.bfloat16
I32 = mybir.dt.int32
U32 = mybir.dt.uint32
U16 = mybir.dt.uint16
U8 = mybir.dt.uint8
E4M3 = mybir.dt.float8_e4m3fn_x4
E5M2 = mybir.dt.float8_e5m2_x4
E2M1 = mybir.dt.float4_e2m1fn_x4
COPY = mybir.ActivationFunctionType.Copy
MAX = mybir.AluOpType.max

P = 128
PACK = 4


def load_words(nc, tile, words):
    nc.sync.dma_start(out=tile[:].bitcast(I32), in_=words[0].rearrange("p n t -> p (n t)").bitcast(I32))


def load_scales_side_by_side(nc, tile, scales):
    nc.sync.dma_start(
        out=tile[:].bitcast(I32).rearrange("r (q c) -> r q c", q=4),
        in_=scales[0].bitcast(I32).rearrange("(q r) c -> r q c", q=4),
    )


def spread_scales(nc, plane, tile, width):
    for q in range(4):
        nc.vector.tensor_copy(
            out=plane[32 * q : 32 * q + 4, :].bitcast(I32), in_=tile[:, width * q : width * (q + 1)].bitcast(I32)
        )


def load_scales_in_place(nc, tile, cols, scales):
    for q in range(4):
        nc.sync.dma_start(
            out=tile[32 * q : 32 * q + 4, cols].bitcast(I32), in_=scales[0, 4 * q : 4 * q + 4, :].bitcast(I32)
        )


def dealt_views(dst, src, run):
    return (
        dst.rearrange("p (t c i) -> p c t i", t=PACK, i=run),
        src.rearrange("p (c i t) -> p c t i", t=PACK, i=run),
    )


def tile_list_boardweighed_twow_further_plain_kernel(
    tc, xt_words, xt_scales, w_words, w_scales, w2_words, w2_scales, sa, wb_words, wb_scales,
    ws_words, ws_scales, offs, offs2, offs3, offs4, offs5, out,
):
    nc = tc.nc
    with ExitStack() as ctx:
        lists = ctx.enter_context(tc.tile_pool(name="lists", bufs=1))
        sb = ctx.enter_context(tc.tile_pool(name="sb", bufs=1))
        psum = ctx.enter_context(tc.psum_pool(name="psum", bufs=1))

        l1 = lists.tile([P, J // 16], U16, name="l1")
        l2 = lists.tile([P, J // 16], U16, name="l2")
        l3 = lists.tile([P, O // 16], U16, name="l3")
        l4 = lists.tile([P, O // 16], U16, name="l4")
        l5 = lists.tile([P, O // 16], U16, name="l5")

        xw = sb.tile([P, T], U16, name="xw", align_bytes=64)
        xs = sb.tile([P, T], U8, name="xs", align_bytes=64)
        ww = sb.tile([P, R], U32, name="ww", align_bytes=64)
        wsc_rows = sb.tile([4, 4 * R], U8, name="wsc_rows", align_bytes=64)
        wsc = sb.tile([P, R], U8, name="wsc", align_bytes=64)
        w2w = sb.tile([P, R], U32, name="w2w", align_bytes=64)
        late = sb.tile([P, R + 2 * N], U8, name="late", align_bytes=64)
        w2_cols, ws_cols, wb_cols = slice(0, R), slice(R, R + N), slice(R + N, R + 2 * N)
        wbw = sb.tile([P, N], U32, name="wbw", align_bytes=64)
        wsw = sb.tile([P, N], U32, name="wsw", align_bytes=64)
        sat = sb.tile([P, PACK], F32, name="sat", align_bytes=64)

        nc.vector.memset(xs[:, 0 : T // 2].bitcast(I32), 0)
        nc.gpsimd.memset(xs[:, T // 2 : T].bitcast(I32), 0)
        for plane in (wsc, late):
            nc.vector.memset(plane[:].bitcast(I32), 0)

        nc.sync.dma_start(l1[:], offs)
        load_scales_side_by_side(nc, wsc_rows, w_scales)
        nc.sync.dma_start(out=xw[:].bitcast(I32), in_=xt_words[0].bitcast(I32))
        load_words(nc, ww, w_words)
        load_scales_in_place(nc, xs, slice(0, T), xt_scales)
        load_words(nc, w2w, w2_words)
        nc.sync.dma_start(l2[:], offs2)
        load_scales_in_place(nc, late, w2_cols, w2_scales)
        nc.sync.dma_start(l5[:], offs5)
        nc.sync.dma_start(l3[:], offs3)
        nc.sync.dma_start(out=sat[:], in_=sa.rearrange("(p t) u -> p (t u)", t=PACK))
        nc.sync.dma_start(l4[:], offs4)
        load_words(nc, wsw, ws_words)
        load_scales_in_place(nc, late, ws_cols, ws_scales)
        load_words(nc, wbw, wb_words)
        load_scales_in_place(nc, late, wb_cols, wb_scales)

        xgw = sb.tile([P, J], U16, name="xgw", align_bytes=64)
        xgs = sb.tile([P, J], U8, name="xgs", align_bytes=64)
        wd = sb.tile([P, R], U32, name="wd", align_bytes=64)
        wds = sb.tile([P, R], U8, name="wds", align_bytes=64)
        w2d = sb.tile([P, R], U32, name="w2d", tag="w2d_then_x5w", align_bytes=64)
        w2ds = sb.tile([P, R], U8, name="w2ds", align_bytes=64)

        spread_scales(nc, wsc, wsc_rows, R)
        dst, src = dealt_views(wds[:], wsc[:], 16)
        nc.vector.tensor_copy(out=dst[:, :, 0:2, :], in_=src[:, :, 0:2, :])
        nc.gpsimd.tensor_copy(out=dst[:, :, 2:4, :], in_=src[:, :, 2:4, :])
        nc.vector.tensor_copy(xgw[:], xw[:].indirect(l1[:]))
        nc.vector.tensor_copy(xgs[:], xs[:].indirect(l1[:]))
        dst, src = dealt_views(wd[:], ww[:], 4)
        nc.scalar.copy(out=dst[:, :, 0:2, :], in_=src[:, :, 0:2, :])
        nc.scalar.copy(out=dst[:, :, 2:4, :], in_=src[:, :, 2:4, :])
        dst, src = dealt_views(w2d[:], w2w[:], 4)
        nc.scalar.copy(out=dst[:, :, 0:2, :], in_=src[:, :, 0:2, :])
        nc.gpsimd.tensor_copy(out=dst[:, :, 2:4, :], in_=src[:, :, 2:4, :])
        dst, src = dealt_views(w2ds[:], late[:, w2_cols], 16)
        nc.gpsimd.tensor_copy(out=dst[:, :, 0:2, :], in_=src[:, :, 0:2, :])
        nc.gpsimd.tensor_copy(out=dst[:, :, 2:4, :], in_=src[:, :, 2:4, :])

        a_ps = [psum.tile([P, J], F32, name="a_ps%d" % t) for t in range(PACK)]
        b_ps = [psum.tile([P, 2 * J], F32, name="b_ps%d" % h) for h in range(2)]
        y_ps = [psum.tile([P, O], F32, name="y_ps%d" % h) for h in range(2)]
        for t in range(PACK):
            cols = slice(P * t, P * (t + 1))
            nc.tensor.matmul_mx(
                out=a_ps[t][:], lhsT=wd[:, cols].bitcast(E5M2), lhsT_scale=wds[:, cols],
                rhs=xgw[:].bitcast(E2M1), rhs_scale=xgs[:], start=True, stop=True,
            )
        for t in range(PACK):
            cols = slice(P * t, P * (t + 1))
            nc.tensor.matmul_mx(
                out=b_ps[t // 2][:, J * (t % 2) : J * (t % 2 + 1)], lhsT=w2d[:, cols].bitcast(E4M3),
                lhsT_scale=w2ds[:, cols], rhs=xgw[:].bitcast(E2M1), rhs_scale=xgs[:], start=True, stop=True,
            )

        board = [sb.tile([P, C], F32, name="board%d" % t, align_bytes=64) for t in range(PACK)]
        for t in range(PACK):
            nc.vector.memset(board[t][:], 0.0)

        a_sb = [sb.tile([P, J], F32, name="a_sb%d" % t, align_bytes=64) for t in range(PACK)]
        b_sb = [sb.tile([P, 2 * J], F32, name="b_sb%d" % h, align_bytes=64) for h in range(2)]
        picked_a = sb.tile([P, PACK, O], F32, name="picked_a", align_bytes=64)
        picked_b = sb.tile([P, PACK, O], F32, name="picked_b", align_bytes=64)

        for t in (0, 2):
            nc.vector.tensor_copy(out=a_sb[t][:], in_=a_ps[t][:])
            nc.scalar.copy(out=a_sb[t + 1][:], in_=a_ps[t + 1][:])
        for t in (0, 2):
            nc.vector.tensor_copy(board[t][:].indirect(l2[:]), a_sb[t][:])
            nc.scalar.activation(board[t + 1][:].indirect(l2[:]), a_sb[t + 1][:], COPY)
        for h in range(2):
            nc.vector.tensor_copy(out=b_sb[h][:], in_=b_ps[h][:])
        for t in (1, 3, 0, 2):
            nc.scalar.activation(picked_a[:, t, :], board[t][:].indirect(l3[:]), COPY, scale=sat[:, t : t + 1])
        for u in range(2):
            window = slice(J * u, J * (u + 1))
            nc.scalar.activation(picked_b[:, u, :], b_sb[0][:, window].indirect(l4[:]), COPY)
            nc.vector.tensor_copy(picked_b[:, 2 + u, :], b_sb[1][:, window].indirect(l4[:]))

        x5w = sb.tile([P, O], U16, name="x5w", tag="w2d_then_x5w", align_bytes=64)
        x5s = sb.tile([P, O], U8, name="x5s", tag="b_sb1", align_bytes=64)
        nc.vector.tensor_copy(x5w[:], xw[:].indirect(l5[:]))
        nc.vector.tensor_copy(x5s[:], xs[:].indirect(l5[:]))
        for h in range(2):
            cols = slice(P * h, P * (h + 1))
            nc.tensor.matmul_mx(
                out=y_ps[h][:], lhsT=wsw[:, cols].bitcast(E4M3), lhsT_scale=late[:, R + P * h : R + P * (h + 1)],
                rhs=x5w[:].bitcast(E2M1), rhs_scale=x5s[:], start=True, stop=False,
            )

        hid = sb.tile([P, O * PACK], BF16, name="hid", align_bytes=64)
        hq = sb.tile([P, O], U32, name="hq", align_bytes=64)
        hs = sb.tile([P, O], U8, name="hs", align_bytes=64)
        halves = (slice(0, O // 2), slice(O // 2, O))
        for half in halves:
            nc.vector.tensor_tensor(
                out=hid[:, PACK * half.start : PACK * half.stop].rearrange("p (c i t) -> p c t i", i=2, t=PACK),
                in0=picked_a[:, :, half].rearrange("p t (c i) -> p c t i", i=2),
                in1=picked_b[:, :, half].rearrange("p t (c i) -> p c t i", i=2),
                op=MAX,
            )
        for half in halves:
            nc.vector.quantize_mx(
                out=hq[:, half].bitcast(E5M2), scales=hs[:, half], in_=hid[:, PACK * half.start : PACK * half.stop]
            )

        y_sb = [sb.tile([P, O], F32, name="y_sb%d" % h, align_bytes=64) for h in range(2)]
        for h in range(2):
            cols = slice(P * h, P * (h + 1))
            nc.tensor.matmul_mx(
                out=y_ps[h][:], lhsT=wbw[:, cols].bitcast(E4M3), lhsT_scale=late[:, R + N + P * h : R + N + P * (h + 1)],
                rhs=hq[:].bitcast(E5M2), rhs_scale=hs[:], start=False, stop=True,
            )
        nc.vector.tensor_copy(out=y_sb[0][:], in_=y_ps[0][:])
        nc.sync.dma_start(out=out[0:P, :], in_=y_sb[0][:])
        nc.scalar.copy(out=y_sb[1][:], in_=y_ps[1][:])
        nc.scalar.dma_start(out=out[P : 2 * P, :], in_=y_sb[1][:])
